import numpy as np, ml_dtypes
CORES = [22,38,54,62,70,110,23,39,55,63,71,111]
N = 12
import mx_ref
NC = 512
CNT = [[64,112,16,80,16,0,0,0,112,64,48,0],[16,64,48,0,80,96,0,0,112,0,80,16],[48,16,64,0,0,80,64,48,16,64,0,112],[48,0,0,16,16,0,96,80,48,96,96,16],[0,0,80,96,80,64,80,16,48,16,32,0],[0,144,32,32,16,16,0,0,16,144,0,112],[64,16,224,64,0,0,16,0,0,0,16,112],[16,16,0,16,0,32,96,16,96,0,112,112],[112,0,32,80,96,48,32,16,0,64,16,16],[96,112,16,0,0,0,16,240,0,0,16,16],[48,0,0,0,64,176,48,0,64,16,96,0],[0,32,0,128,144,0,64,96,0,48,0,0]]
OFF = [[sum(c[:e]) for e in range(N + 1)] for c in CNT]
BF = ml_dtypes.bfloat16
def setup_inputs(rng):
    def f(*shape):
        return mx_ref.flush((rng.standard_normal(shape, dtype=np.float32) * np.exp2(rng.integers(-2, 3, shape[:-1] + (1,)))).astype(BF))
    return {"w": f(N, 128, 512), "x": f(N, 128, 4 * NC)}
def setup_inputs_blocks(rng):
    d = setup_inputs(rng)
    for k in ("w", "x"): d[k] = mx_ref.spread(d[k], rng, 4)
    return d
def setup_inputs_wide(rng):
    d = setup_inputs(rng)
    for k in ("w", "x"): d[k] = mx_ref.flush((d[k].astype(np.float32) * np.exp2(rng.integers(-8, 9, (N, 1, 1))).astype(np.float32)).astype(BF))
    return d
def setup_inputs_zeros(rng):
    d = setup_inputs(rng); v = d["x"].reshape(N, 128, -1, 4).copy()
    v[np.broadcast_to((rng.random((N, 1, v.shape[2], 1)) < 0.33), v.shape)] = 0
    d["x"] = v.reshape(d["x"].shape)
    return d
def reference(w, x):
    y = np.zeros((N, 128, NC), np.float32)
    for e in range(N):
        t = np.concatenate([x[j][:, 4 * OFF[j][e]:4 * OFF[j][e + 1]] for j in range(N)], axis=1)
        p = mx_ref.matmul(mx_ref.quantize(w[e]), mx_ref.quantize(t)); c = 0
        for j in range(N):
            a, b = OFF[j][e], OFF[j][e + 1]
            y[j][:, a:b] = p[:, c:c + b - a]; c += b - a
    return {"y": y}

@@ -1,0 +1,245 @@
+from concourse.bass import DstId, RemoteDMATransfer
+from concourse.mybir import dt
+
+FWD = "batch"
+HELP = False
+
+NSLOT = 12
+WCOL = 128
+NTOK = 512
+MINWIN = 128
+NBANK = 8
+
+SCRATCH = {
+    "wb": ("sbuf", [128, 4 * WCOL], "bfloat16"),
+    "xb": ("sbuf", [128, 4 * NTOK], "bfloat16"),
+    "wq": ("sbuf", [128, WCOL * NSLOT], "float8_e4m3fn_x4"),
+    "ws": ("sbuf", [128, WCOL * NSLOT], "uint8"),
+    "xq": ("sbuf", [128, NTOK], "float8_e4m3fn_x4"),
+    "xs": ("sbuf", [128, NTOK], "uint8"),
+    "ps": ("psum", [128, 512 * NBANK], "float32"),
+    "yb": ("sbuf", [128, NTOK], "float32"),
+}
+SEMAPHORES = ["a%d" % e for e in range(12)] + ["fw0", "fw1", "lw", "lx", "qw", "qx", "mm", "cp", "st", "loc"]
+
+
+def make_plan(cores, CNT, topo):
+    N = len(cores)
+    chip_of = [topo.chip(c) for c in cores]
+    chips = sorted(set(chip_of))
+    nch = len(chips)
+    members = {C: [r for r in range(N) if chip_of[r] == C] for C in chips}
+    allc = [c for c in range(topo.CHIPS * topo.CORES_PER_CHIP)]
+    both, single, local = {}, {}, {}
+    for e in range(N):
+        s = chips.index(chip_of[e])
+        p = members[chip_of[e]].index(e)
+        walk = [chips[(s + k) % nch] for k in range(1, nch)]
+        if p % 2:
+            walk.reverse()
+        both[e], single[e] = [], []
+        for C in walk:
+            nd = [r for r in members[C] if CNT[r][e] > 0]
+            if len(nd) > 1 and FWD != "none":
+                both[e].append(nd)
+            else:
+                for r in nd:
+                    single[e].append(r)
+        local[e] = [r for r in members[chip_of[e]] if r != e and CNT[r][e] > 0]
+    nfwd = [0] * N
+    recv = {}
+    maxb = max(len(both[e]) for e in range(N))
+    for k in range(maxb):
+        for e in range(N):
+            if k < len(both[e]):
+                nd = both[e][k]
+                r = min(nd, key=lambda q: (nfwd[q], (q + e) % 2))
+                nfwd[r] += 1
+                recv[(e, k)] = (r, [q for q in nd if q != r])
+    helper, hlist = {}, {}
+    if HELP:
+        used = set(cores)
+        for e in range(N):
+            n = len(both[e]) + len(single[e])
+            h = min(2 if n >= 5 else 1, len(single[e]))
+            if h == 0:
+                continue
+            take = single[e][len(single[e]) - h:]
+            cand = [c for c in allc if topo.chip(c) == chip_of[e] and c not in used
+                    and topo.die(c) != topo.die(cores[e])
+                    and all(topo.may_write(c, cores[r]) for r in take)]
+            if not cand:
+                continue
+            helper[e] = cand[0]
+            used.add(cand[0])
+            hlist[e] = take
+            single[e] = single[e][:len(single[e]) - h]
+    give = {r: [] for r in range(N)}
+    for k in range(maxb):
+        for e in range(N):
+            if (e, k) in recv:
+                give[recv[(e, k)][0]].append((k, e))
+    slot = {r: {} for r in range(N)}
+    for r in range(N):
+        for (k, e) in give[r]:
+            slot[r][e] = len(slot[r])
+    for r in range(N):
+        for (k, e) in give[r]:
+            for q in recv[(e, k)][1]:
+                slot[q][e] = len(slot[q])
+    for r in range(N):
+        for e in range(N):
+            if (CNT[r][e] > 0 or e == r) and e not in slot[r]:
+                slot[r][e] = len(slot[r])
+    prog = {c: [] for c in cores}
+    key = {r: {} for r in range(N)}
+    sem = {r: {e: "a%d" % e for e in slot[r]} for r in range(N)}
+    for e in range(N):
+        c = cores[e]
+        name = "a%d" % e
+        A = ("lo", slot[e][e], 1, [(cores[recv[(e, k)][0]], slot[recv[(e, k)][0]][e]) for k in range(len(both[e]))], name)
+        B = ("lo", slot[e][e], 1, [(cores[r], slot[r][e]) for r in single[e]], name)
+        L = [(cores[r], slot[r][e]) for r in local[e]]
+        if e in helper:
+            L = [(helper[e], 0)] + L
+        L = ("hi", slot[e][e], 1, L, name)
+        key[e][e] = 0.0
+        for k in range(len(both[e])):
+            key[recv[(e, k)][0]][e] = k + 1.0
+        for i, r in enumerate(single[e]):
+            key[r][e] = len(both[e]) + i + 1.0
+        for r in local[e]:
+            key[r][e] = 1.5
+        if e in helper:
+            for i, r in enumerate(hlist[e]):
+                key[r][e] = 3.0 + i
+            first, second = [A, L], [B]
+        else:
+            first, second = [A], [B, L]
+        first = [t for t in first if t[3]]
+        second = [t for t in second if t[3]]
+        if first:
+            prog[c].append(("send", first))
+        if second:
+            prog[c].append(("send", second))
+        if e in helper:
+            prog[helper[e]] = [("wait", name), ("send", [("lo", 0, 1, [(cores[r], slot[r][e]) for r in hlist[e]], name)])]
+    for r in range(N):
+        if FWD == "each":
+            parts = [(give[r][i:i + 1], None) for i in range(len(give[r]))]
+        elif FWD == "two" and len(give[r]) > 1:
+            parts = [(give[r][:-1], "fw0"), (give[r][-1:], "fw1")]
+        else:
+            parts = [(give[r], "fw0")]
+        for part, name in parts:
+            if not part:
+                continue
+            for (k, e) in part:
+                prog[cores[r]].append(("wait", "a%d" % e))
+            (k0, e0) = part[0]
+            nm = name if name else "a%d" % e0
+            prog[cores[r]].append(("send", [("hi", slot[r][e0], len(part), [(cores[q], slot[q][e0]) for q in recv[(e0, k0)][1]], nm)]))
+            for (k, e) in part:
+                for q in recv[(e, k)][1]:
+                    key[q][e] = part[-1][0] + 2.5
+                    sem[q][e] = nm
+    order = {r: sorted([e for e in range(N) if CNT[r][e] > 0], key=lambda e: (key[r][e], e)) for r in range(N)}
+    return prog, slot, sem, order
+
+
+def _bits(m):
+    return bin(m).count("1")
+
+
+def _mask(topo, cores, core, eng, dsts):
+    lo = topo.mask(core, [c for c in cores if topo.chip(c) != topo.chip(core)][0])
+    m = lo if eng == "lo" else ~lo
+    for (dc, ds) in dsts:
+        m &= topo.mask(core, dc)
+    return m
+
+
+def _expect(topo, cores, prog, core):
+    tot = {}
+    for c in prog:
+        for st in prog[c]:
+            if st[0] == "send":
+                for (eng, s0, ns, dsts, name) in st[1]:
+                    for (dc, ds) in dsts:
+                        if dc == core:
+                            tot[name] = tot.get(name, 0) + 2 * _bits(_mask(topo, cores, c, eng, dsts))
+    return tot
+
+
+def run_steps(g, core, T, topo, prog):
+    cores = list(T.cores)
+    expect = _expect(topo, cores, prog, core)
+    sent = 0
+    for st in prog[core]:
+        if st[0] == "wait":
+            g.wait_ge(T.sem[st[1]], expect[st[1]])
+            continue
+        for kind in ("planes", "codes"):
+            trs = []
+            for (eng, s0, ns, dsts, name) in st[1]:
+                m = _mask(topo, cores, core, eng, dsts)
+                if kind == "planes":
+                    src = T.ws[:, s0 * WCOL:(s0 + ns) * WCOL]
+                    out = [T.ws[:, ds * WCOL:(ds + ns) * WCOL] for (dc, ds) in dsts]
+                else:
+                    src = T.wq[:, s0 * WCOL:(s0 + ns) * WCOL].bitcast(dt.uint8)
+                    out = [T.wq[:, ds * WCOL:(ds + ns) * WCOL].bitcast(dt.uint8) for (dc, ds) in dsts]
+                ids = [DstId(rid=topo.addr(dc)[0], pnc=topo.addr(dc)[1]) for (dc, ds) in dsts]
+                trs.append(RemoteDMATransfer(dst_ids=ids, dma_engine_mask=m, remote_sem=T.sem[name], srcs=[src], dsts=out))
+                sent += _bits(m)
+            g.remote_dma_fused(trs, local_sem=T.sem.loc)
+    if sent:
+        g.wait_ge(T.sem.loc, sent)
+
+
+def rank_program(g, core, T, topo):
+    CNT = T.tables["CNT"]
+    cores = list(T.cores)
+    prog, slot, sem, order = make_plan(cores, CNT, topo)
+    rank = T.rank_of(core)
+    if rank is None:
+        if core in prog:
+            run_steps(g, core, T, topo, prog)
+        return
+    expect = _expect(topo, cores, prog, core)
+    off = [sum(CNT[rank][:e]) for e in range(len(cores) + 1)]
+    mine = slot[rank][rank]
+
+    g.sync.dma_start(T.wb[:], T.w[:]).then_inc(T.sem.lw, 16)
+    g.sync.dma_start(T.xb[:], T.x[:]).then_inc(T.sem.lx, 16)
+
+    g.vector.wait_ge(T.sem.lw, 16)
+    g.vector.quantize_mx(T.wq[:, mine * WCOL:(mine + 1) * WCOL], T.ws[:, mine * WCOL:(mine + 1) * WCOL], T.wb[:]).then_inc(T.sem.qw, 1)
+    g.vector.wait_ge(T.sem.lx, 16)
+    g.vector.quantize_mx(T.xq[:], T.xs[:], T.xb[:]).then_inc(T.sem.qx, 1)
+
+    g.wait_ge(T.sem.qw, 1)
+    run_steps(g, core, T, topo, prog)
+
+    g.tensor.wait_ge(T.sem.qx, 1)
+    todo = order[rank]
+    for k, e in enumerate(todo):
+        a, n = off[e], CNT[rank][e]
+        w0 = a if n >= MINWIN else min(a, NTOK - MINWIN)
+        wn = max(n, MINWIN)
+        s = slot[rank][e]
+        b = (k % NBANK) * 512
+        if e == rank:
+            g.tensor.wait_ge(T.sem.qw, 1)
+        else:
+            g.tensor.wait_ge(T.sem[sem[rank][e]], expect[sem[rank][e]])
+        if k >= NBANK:
+            g.tensor.wait_ge(T.sem.cp, k - NBANK + 1)
+        g.tensor.matmul_mx(T.ps[:, b:b + wn], T.wq[:, s * WCOL:(s + 1) * WCOL], T.ws[:, s * WCOL:(s + 1) * WCOL],
+                           T.xq[:, w0:w0 + wn], T.xs[:, w0:w0 + wn], True, True).then_inc(T.sem.mm, 1)
+        g.vector.wait_ge(T.sem.mm, k + 1)
+        g.vector.tensor_copy(T.yb[:, a:a + n], T.ps[:, b + a - w0:b + a - w0 + n]).then_inc(T.sem.cp, 1)
+
+    g.sync.wait_ge(T.sem.cp, len(todo))
+    g.sync.dma_start(T.y[:], T.yb[:]).then_inc(T.sem.st, 16)
+    g.sync.wait_ge(T.sem.st, 16)

@@ -1,26 +1,26 @@
 from concourse.bass import DstId, RemoteDMATransfer
 from concourse.mybir import dt
 
-FWD = "batch"
-HELP = False
-
-NSLOT = 12
 WCOL = 128
 NTOK = 512
 MINWIN = 128
 NBANK = 8
+NEXP = 12
+LATE = 2
+
+T_PLANE, T_CODES, T_HOP = 20, 32, 20
 
 SCRATCH = {
     "wb": ("sbuf", [128, 4 * WCOL], "bfloat16"),
     "xb": ("sbuf", [128, 4 * NTOK], "bfloat16"),
-    "wq": ("sbuf", [128, WCOL * NSLOT], "float8_e4m3fn_x4"),
-    "ws": ("sbuf", [128, WCOL * NSLOT], "uint8"),
+    "wq": ("sbuf", [128, WCOL * NEXP], "float8_e4m3fn_x4"),
+    "ws": ("sbuf", [128, WCOL * NEXP], "uint8"),
     "xq": ("sbuf", [128, NTOK], "float8_e4m3fn_x4"),
     "xs": ("sbuf", [128, NTOK], "uint8"),
     "ps": ("psum", [128, 512 * NBANK], "float32"),
     "yb": ("sbuf", [128, NTOK], "float32"),
 }
-SEMAPHORES = ["a%d" % e for e in range(12)] + ["fw0", "fw1", "lw", "lx", "qw", "qx", "mm", "cp", "st", "loc"]
+SEMAPHORES = ["a%d" % e for e in range(NEXP)] + ["hp", "lw", "lx", "qw", "qx", "mm", "cp", "st", "loc"]
 
 
 def make_plan(cores, CNT, topo):
@@ -29,122 +29,62 @@ def make_plan(cores, CNT, topo):
     chips = sorted(set(chip_of))
     nch = len(chips)
     members = {C: [r for r in range(N) if chip_of[r] == C] for C in chips}
-    allc = [c for c in range(topo.CHIPS * topo.CORES_PER_CHIP)]
-    both, single, local = {}, {}, {}
+    allc = list(range(topo.CHIPS * topo.CORES_PER_CHIP))
+    off = {e: [r for r in range(N) if chip_of[r] != chip_of[e] and CNT[r][e] > 0] for e in range(N)}
+    sib = {e: [r for r in range(N) if chip_of[r] == chip_of[e] and r != e and CNT[r][e] > 0] for e in range(N)}
+    used = set(cores)
+    h1, h2 = {}, {}
     for e in range(N):
-        s = chips.index(chip_of[e])
-        p = members[chip_of[e]].index(e)
-        walk = [chips[(s + k) % nch] for k in range(1, nch)]
-        if p % 2:
-            walk.reverse()
-        both[e], single[e] = [], []
-        for C in walk:
-            nd = [r for r in members[C] if CNT[r][e] > 0]
-            if len(nd) > 1 and FWD != "none":
-                both[e].append(nd)
-            else:
-                for r in nd:
-                    single[e].append(r)
-        local[e] = [r for r in members[chip_of[e]] if r != e and CNT[r][e] > 0]
-    nfwd = [0] * N
-    recv = {}
-    maxb = max(len(both[e]) for e in range(N))
-    for k in range(maxb):
-        for e in range(N):
-            if k < len(both[e]):
-                nd = both[e][k]
-                r = min(nd, key=lambda q: (nfwd[q], (q + e) % 2))
-                nfwd[r] += 1
-                recv[(e, k)] = (r, [q for q in nd if q != r])
-    helper, hlist = {}, {}
-    if HELP:
-        used = set(cores)
-        for e in range(N):
-            n = len(both[e]) + len(single[e])
-            h = min(2 if n >= 5 else 1, len(single[e]))
-            if h == 0:
-                continue
-            take = single[e][len(single[e]) - h:]
-            cand = [c for c in allc if topo.chip(c) == chip_of[e] and c not in used
-                    and topo.die(c) != topo.die(cores[e])
-                    and all(topo.may_write(c, cores[r]) for r in take)]
-            if not cand:
-                continue
-            helper[e] = cand[0]
+        cand = [h for h in allc if topo.chip(h) == chip_of[e] and h not in used and topo.die(h) != topo.die(cores[e])
+                and all(topo.may_write(h, cores[r]) for r in off[e])]
+        if cand and len(off[e]) > 1:
+            h1[e] = cand[0]
             used.add(cand[0])
-            hlist[e] = take
-            single[e] = single[e][:len(single[e]) - h]
-    give = {r: [] for r in range(N)}
-    for k in range(maxb):
-        for e in range(N):
-            if (e, k) in recv:
-                give[recv[(e, k)][0]].append((k, e))
-    slot = {r: {} for r in range(N)}
-    for r in range(N):
-        for (k, e) in give[r]:
-            slot[r][e] = len(slot[r])
-    for r in range(N):
-        for (k, e) in give[r]:
-            for q in recv[(e, k)][1]:
-                slot[q][e] = len(slot[q])
-    for r in range(N):
-        for e in range(N):
-            if (CNT[r][e] > 0 or e == r) and e not in slot[r]:
-                slot[r][e] = len(slot[r])
-    prog = {c: [] for c in cores}
-    key = {r: {} for r in range(N)}
-    sem = {r: {e: "a%d" % e for e in slot[r]} for r in range(N)}
+    for e in range(N):
+        p = members[chip_of[e]].index(e)
+        cand = [h for h in allc if topo.chip(h) == chip_of[e] and h not in used
+                and any(topo.may_write(h, cores[r]) for r in off[e])]
+        cand.sort(key=lambda h: ((topo.die(h) != topo.die(cores[e])) != (p % 2 == 1), h))
+        if cand and e in h1 and len(off[e]) > 3:
+            h2[e] = cand[0]
+            used.add(cand[0])
+    prog = {}
+    key = {r: {r: 0} for r in range(N)}
     for e in range(N):
         c = cores[e]
         name = "a%d" % e
-        A = ("lo", slot[e][e], 1, [(cores[recv[(e, k)][0]], slot[recv[(e, k)][0]][e]) for k in range(len(both[e]))], name)
-        B = ("lo", slot[e][e], 1, [(cores[r], slot[r][e]) for r in single[e]], name)
-        L = [(cores[r], slot[r][e]) for r in local[e]]
-        if e in helper:
-            L = [(helper[e], 0)] + L
-        L = ("hi", slot[e][e], 1, L, name)
-        key[e][e] = 0.0
-        for k in range(len(both[e])):
-            key[recv[(e, k)][0]][e] = k + 1.0
-        for i, r in enumerate(single[e]):
-            key[r][e] = len(both[e]) + i + 1.0
-        for r in local[e]:
-            key[r][e] = 1.5
-        if e in helper:
-            for i, r in enumerate(hlist[e]):
-                key[r][e] = 3.0 + i
-            first, second = [A, L], [B]
-        else:
-            first, second = [A], [B, L]
-        first = [t for t in first if t[3]]
-        second = [t for t in second if t[3]]
-        if first:
-            prog[c].append(("send", first))
-        if second:
-            prog[c].append(("send", second))
-        if e in helper:
-            prog[helper[e]] = [("wait", name), ("send", [("lo", 0, 1, [(cores[r], slot[r][e]) for r in hlist[e]], name)])]
-    for r in range(N):
-        if FWD == "each":
-            parts = [(give[r][i:i + 1], None) for i in range(len(give[r]))]
-        elif FWD == "two" and len(give[r]) > 1:
-            parts = [(give[r][:-1], "fw0"), (give[r][-1:], "fw1")]
-        else:
-            parts = [(give[r], "fw0")]
-        for part, name in parts:
-            if not part:
-                continue
-            for (k, e) in part:
-                prog[cores[r]].append(("wait", "a%d" % e))
-            (k0, e0) = part[0]
-            nm = name if name else "a%d" % e0
-            prog[cores[r]].append(("send", [("hi", slot[r][e0], len(part), [(cores[q], slot[q][e0]) for q in recv[(e0, k0)][1]], nm)]))
-            for (k, e) in part:
-                for q in recv[(e, k)][1]:
-                    key[q][e] = part[-1][0] + 2.5
-                    sem[q][e] = nm
+        s = chips.index(chip_of[e])
+        p = members[chip_of[e]].index(e)
+        senders = [c] + [h[e] for h in (h1, h2) if e in h]
+        start = {c: 2 * T_PLANE + T_HOP}
+        step = {c: T_PLANE + T_CODES}
+        for k, h in enumerate(senders[1:]):
+            start[h] = 2 * T_PLANE + (k + 1) * T_CODES + 2 * T_HOP
+            step[h] = T_CODES
+        lists = {q: [] for q in senders}
+        todo = sorted(off[e], key=lambda r: (sum(1 for q in senders if topo.may_write(q, cores[r])), r))
+        for r in todo:
+            ok = [q for q in senders if topo.may_write(q, cores[r])]
+            q = min(ok, key=lambda q: (start[q] + step[q] * (len(lists[q]) + 1), senders.index(q)))
+            lists[q].append(r)
+        for i, q in enumerate(senders):
+            lists[q].sort(key=lambda r: (((chips.index(chip_of[r]) - s) * (1 if p % 2 == 0 else -1) + i) % nch, r))
+            for k, r in enumerate(lists[q]):
+                key[r][e] = start[q] + step[q] * (k + 1)
+        helpers = [h for h in senders[1:] if lists[h]]
+        for r in sib[e]:
+            key[r][e] = 2 * T_PLANE + (len(helpers) + 1) * T_CODES
+        mine = [cores[r] for r in lists[c]]
+        near = [cores[r] for r in sib[e]]
+        P = [("hi", helpers, "hp"), ("lo", mine + near, name)]
+        C = [("hi", helpers + near, name), ("lo", mine, name)]
+        prog[c] = [("send", "planes", e, [t for t in P if t[1]]), ("send", "codes", e, [t for t in C if t[1]])]
+        for h in helpers:
+            d = [cores[r] for r in lists[h]]
+            prog[h] = [("wait", "hp"), ("send", "planes", e, [("lo", d, name)]),
+                       ("wait", name), ("send", "codes", e, [("lo", d, name)])]
     order = {r: sorted([e for e in range(N) if CNT[r][e] > 0], key=lambda e: (key[r][e], e)) for r in range(N)}
-    return prog, slot, sem, order
+    return prog, order
 
 
 def _bits(m):
@@ -154,8 +94,8 @@ def _bits(m):
 def _mask(topo, cores, core, eng, dsts):
     lo = topo.mask(core, [c for c in cores if topo.chip(c) != topo.chip(core)][0])
     m = lo if eng == "lo" else ~lo
-    for (dc, ds) in dsts:
-        m &= topo.mask(core, dc)
+    for d in dsts:
+        m &= topo.mask(core, d)
     return m
 
 
@@ -164,10 +104,9 @@ def _expect(topo, cores, prog, core):
     for c in prog:
         for st in prog[c]:
             if st[0] == "send":
-                for (eng, s0, ns, dsts, name) in st[1]:
-                    for (dc, ds) in dsts:
-                        if dc == core:
-                            tot[name] = tot.get(name, 0) + 2 * _bits(_mask(topo, cores, c, eng, dsts))
+                for (eng, dsts, name) in st[3]:
+                    if core in dsts:
+                        tot[name] = tot.get(name, 0) + _bits(_mask(topo, cores, c, eng, dsts))
     return tot
 
 
@@ -179,20 +118,18 @@ def run_steps(g, core, T, topo, prog):
         if st[0] == "wait":
             g.wait_ge(T.sem[st[1]], expect[st[1]])
             continue
-        for kind in ("planes", "codes"):
-            trs = []
-            for (eng, s0, ns, dsts, name) in st[1]:
-                m = _mask(topo, cores, core, eng, dsts)
-                if kind == "planes":
-                    src = T.ws[:, s0 * WCOL:(s0 + ns) * WCOL]
-                    out = [T.ws[:, ds * WCOL:(ds + ns) * WCOL] for (dc, ds) in dsts]
-                else:
-                    src = T.wq[:, s0 * WCOL:(s0 + ns) * WCOL].bitcast(dt.uint8)
-                    out = [T.wq[:, ds * WCOL:(ds + ns) * WCOL].bitcast(dt.uint8) for (dc, ds) in dsts]
-                ids = [DstId(rid=topo.addr(dc)[0], pnc=topo.addr(dc)[1]) for (dc, ds) in dsts]
-                trs.append(RemoteDMATransfer(dst_ids=ids, dma_engine_mask=m, remote_sem=T.sem[name], srcs=[src], dsts=out))
-                sent += _bits(m)
-            g.remote_dma_fused(trs, local_sem=T.sem.loc)
+        kind, e = st[1], st[2]
+        if kind == "planes":
+            ap = T.ws[:, e * WCOL:(e + 1) * WCOL]
+        else:
+            ap = T.wq[:, e * WCOL:(e + 1) * WCOL].bitcast(dt.uint8)
+        trs = []
+        for (eng, dsts, name) in st[3]:
+            m = _mask(topo, cores, core, eng, dsts)
+            ids = [DstId(rid=topo.addr(d)[0], pnc=topo.addr(d)[1]) for d in dsts]
+            trs.append(RemoteDMATransfer(dst_ids=ids, dma_engine_mask=m, remote_sem=T.sem[name], srcs=[ap], dsts=[ap for d in dsts]))
+            sent += _bits(m)
+        g.remote_dma_fused(trs, local_sem=T.sem.loc)
     if sent:
         g.wait_ge(T.sem.loc, sent)
 
@@ -200,7 +137,7 @@ def run_steps(g, core, T, topo, prog):
 def rank_program(g, core, T, topo):
     CNT = T.tables["CNT"]
     cores = list(T.cores)
-    prog, slot, sem, order = make_plan(cores, CNT, topo)
+    prog, order = make_plan(cores, CNT, topo)
     rank = T.rank_of(core)
     if rank is None:
         if core in prog:
@@ -208,13 +145,12 @@ def rank_program(g, core, T, topo):
         return
     expect = _expect(topo, cores, prog, core)
     off = [sum(CNT[rank][:e]) for e in range(len(cores) + 1)]
-    mine = slot[rank][rank]
 
     g.sync.dma_start(T.wb[:], T.w[:]).then_inc(T.sem.lw, 16)
     g.sync.dma_start(T.xb[:], T.x[:]).then_inc(T.sem.lx, 16)
 
     g.vector.wait_ge(T.sem.lw, 16)
-    g.vector.quantize_mx(T.wq[:, mine * WCOL:(mine + 1) * WCOL], T.ws[:, mine * WCOL:(mine + 1) * WCOL], T.wb[:]).then_inc(T.sem.qw, 1)
+    g.vector.quantize_mx(T.wq[:, rank * WCOL:(rank + 1) * WCOL], T.ws[:, rank * WCOL:(rank + 1) * WCOL], T.wb[:]).then_inc(T.sem.qw, 1)
     g.vector.wait_ge(T.sem.lx, 16)
     g.vector.quantize_mx(T.xq[:], T.xs[:], T.xb[:]).then_inc(T.sem.qx, 1)
 
@@ -227,19 +163,31 @@ def rank_program(g, core, T, topo):
         a, n = off[e], CNT[rank][e]
         w0 = a if n >= MINWIN else min(a, NTOK - MINWIN)
         wn = max(n, MINWIN)
-        s = slot[rank][e]
         b = (k % NBANK) * 512
         if e == rank:
             g.tensor.wait_ge(T.sem.qw, 1)
         else:
-            g.tensor.wait_ge(T.sem[sem[rank][e]], expect[sem[rank][e]])
+            g.tensor.wait_ge(T.sem["a%d" % e], expect["a%d" % e])
         if k >= NBANK:
             g.tensor.wait_ge(T.sem.cp, k - NBANK + 1)
-        g.tensor.matmul_mx(T.ps[:, b:b + wn], T.wq[:, s * WCOL:(s + 1) * WCOL], T.ws[:, s * WCOL:(s + 1) * WCOL],
+        g.tensor.matmul_mx(T.ps[:, b:b + wn], T.wq[:, e * WCOL:(e + 1) * WCOL], T.ws[:, e * WCOL:(e + 1) * WCOL],
                            T.xq[:, w0:w0 + wn], T.xs[:, w0:w0 + wn], True, True).then_inc(T.sem.mm, 1)
         g.vector.wait_ge(T.sem.mm, k + 1)
         g.vector.tensor_copy(T.yb[:, a:a + n], T.ps[:, b + a - w0:b + a - w0 + n]).then_inc(T.sem.cp, 1)
 
-    g.sync.wait_ge(T.sem.cp, len(todo))
-    g.sync.dma_start(T.y[:], T.yb[:]).then_inc(T.sem.st, 16)
-    g.sync.wait_ge(T.sem.st, 16)
+    nlate = min(LATE, len(todo) - 1)
+    early = sorted(todo[:len(todo) - nlate])
+    runs = []
+    for e in early:
+        if runs and runs[-1][1] == off[e]:
+            runs[-1][1] = off[e + 1]
+        else:
+            runs.append([off[e], off[e + 1]])
+    g.sync.wait_ge(T.sem.cp, len(early))
+    for (a, b) in runs:
+        g.sync.dma_start(T.y[:, a:b], T.yb[:, a:b]).then_inc(T.sem.st, 16)
+    for i in range(nlate):
+        e = todo[len(early) + i]
+        g.sync.wait_ge(T.sem.cp, len(early) + i + 1)
+        g.sync.dma_start(T.y[:, off[e]:off[e + 1]], T.yb[:, off[e]:off[e + 1]]).then_inc(T.sem.st, 16)
+    g.sync.wait_ge(T.sem.st, 16 * (len(runs) + nlate))

@@ -1,26 +1,28 @@
 from concourse.bass import DstId, RemoteDMATransfer
 from concourse.mybir import dt
 
+FWD = "two"
+HELP = True
+LATE = 4
+
+NSLOT = 12
 WCOL = 128
 NTOK = 512
 MINWIN = 128
 NBANK = 8
-NEXP = 12
-LATE = 2
-
-T_PLANE, T_CODES, T_HOP = 20, 32, 20
+BOTH = ("planes", "codes")
 
 SCRATCH = {
     "wb": ("sbuf", [128, 4 * WCOL], "bfloat16"),
     "xb": ("sbuf", [128, 4 * NTOK], "bfloat16"),
-    "wq": ("sbuf", [128, WCOL * NEXP], "float8_e4m3fn_x4"),
-    "ws": ("sbuf", [128, WCOL * NEXP], "uint8"),
+    "wq": ("sbuf", [128, WCOL * NSLOT], "float8_e4m3fn_x4"),
+    "ws": ("sbuf", [128, WCOL * NSLOT], "uint8"),
     "xq": ("sbuf", [128, NTOK], "float8_e4m3fn_x4"),
     "xs": ("sbuf", [128, NTOK], "uint8"),
     "ps": ("psum", [128, 512 * NBANK], "float32"),
     "yb": ("sbuf", [128, NTOK], "float32"),
 }
-SEMAPHORES = ["a%d" % e for e in range(NEXP)] + ["hp", "lw", "lx", "qw", "qx", "mm", "cp", "st", "loc"]
+SEMAPHORES = ["a%d" % e for e in range(12)] + ["hp", "fw0", "fw1", "lw", "lx", "qw", "qx", "mm", "cp", "st", "loc"]
 
 
 def make_plan(cores, CNT, topo):
@@ -29,62 +31,122 @@ def make_plan(cores, CNT, topo):
     chips = sorted(set(chip_of))
     nch = len(chips)
     members = {C: [r for r in range(N) if chip_of[r] == C] for C in chips}
-    allc = list(range(topo.CHIPS * topo.CORES_PER_CHIP))
-    off = {e: [r for r in range(N) if chip_of[r] != chip_of[e] and CNT[r][e] > 0] for e in range(N)}
-    sib = {e: [r for r in range(N) if chip_of[r] == chip_of[e] and r != e and CNT[r][e] > 0] for e in range(N)}
-    used = set(cores)
-    h1, h2 = {}, {}
+    allc = [c for c in range(topo.CHIPS * topo.CORES_PER_CHIP)]
+    both, single, local = {}, {}, {}
     for e in range(N):
-        cand = [h for h in allc if topo.chip(h) == chip_of[e] and h not in used and topo.die(h) != topo.die(cores[e])
-                and all(topo.may_write(h, cores[r]) for r in off[e])]
-        if cand and len(off[e]) > 1:
-            h1[e] = cand[0]
-            used.add(cand[0])
-    for e in range(N):
+        s = chips.index(chip_of[e])
         p = members[chip_of[e]].index(e)
-        cand = [h for h in allc if topo.chip(h) == chip_of[e] and h not in used
-                and any(topo.may_write(h, cores[r]) for r in off[e])]
-        cand.sort(key=lambda h: ((topo.die(h) != topo.die(cores[e])) != (p % 2 == 1), h))
-        if cand and e in h1 and len(off[e]) > 3:
-            h2[e] = cand[0]
+        walk = [chips[(s + k) % nch] for k in range(1, nch)]
+        if p % 2:
+            walk.reverse()
+        both[e], single[e] = [], []
+        for C in walk:
+            nd = [r for r in members[C] if CNT[r][e] > 0]
+            if len(nd) > 1 and FWD != "none":
+                both[e].append(nd)
+            else:
+                for r in nd:
+                    single[e].append(r)
+        local[e] = [r for r in members[chip_of[e]] if r != e and CNT[r][e] > 0]
+    nfwd = [0] * N
+    recv = {}
+    maxb = max(len(both[e]) for e in range(N))
+    for k in range(maxb):
+        for e in range(N):
+            if k < len(both[e]):
+                nd = both[e][k]
+                r = min(nd, key=lambda q: (nfwd[q], (q + e) % 2))
+                nfwd[r] += 1
+                recv[(e, k)] = (r, [q for q in nd if q != r])
+    helper, hlist = {}, {}
+    if HELP:
+        used = set(cores)
+        for e in range(N):
+            n = len(both[e]) + len(single[e])
+            h = min(2 if n >= 5 else 1, len(single[e]))
+            if h == 0:
+                continue
+            take = single[e][len(single[e]) - h:]
+            cand = [c for c in allc if topo.chip(c) == chip_of[e] and c not in used
+                    and topo.die(c) != topo.die(cores[e])
+                    and all(topo.may_write(c, cores[r]) for r in take)]
+            if not cand:
+                continue
+            helper[e] = cand[0]
             used.add(cand[0])
-    prog = {}
-    key = {r: {r: 0} for r in range(N)}
+            hlist[e] = take
+            single[e] = single[e][:len(single[e]) - h]
+    give = {r: [] for r in range(N)}
+    for k in range(maxb):
+        for e in range(N):
+            if (e, k) in recv:
+                give[recv[(e, k)][0]].append((k, e))
+    slot = {r: {} for r in range(N)}
+    for r in range(N):
+        for (k, e) in give[r]:
+            slot[r][e] = len(slot[r])
+    for r in range(N):
+        for (k, e) in give[r]:
+            for q in recv[(e, k)][1]:
+                slot[q][e] = len(slot[q])
+    for r in range(N):
+        for e in range(N):
+            if (CNT[r][e] > 0 or e == r) and e not in slot[r]:
+                slot[r][e] = len(slot[r])
+    prog = {c: [] for c in cores}
+    key = {r: {} for r in range(N)}
+    sem = {r: {e: ["a%d" % e] for e in slot[r]} for r in range(N)}
     for e in range(N):
         c = cores[e]
         name = "a%d" % e
-        s = chips.index(chip_of[e])
-        p = members[chip_of[e]].index(e)
-        senders = [c] + [h[e] for h in (h1, h2) if e in h]
-        start = {c: 2 * T_PLANE + T_HOP}
-        step = {c: T_PLANE + T_CODES}
-        for k, h in enumerate(senders[1:]):
-            start[h] = 2 * T_PLANE + (k + 1) * T_CODES + 2 * T_HOP
-            step[h] = T_CODES
-        lists = {q: [] for q in senders}
-        todo = sorted(off[e], key=lambda r: (sum(1 for q in senders if topo.may_write(q, cores[r])), r))
-        for r in todo:
-            ok = [q for q in senders if topo.may_write(q, cores[r])]
-            q = min(ok, key=lambda q: (start[q] + step[q] * (len(lists[q]) + 1), senders.index(q)))
-            lists[q].append(r)
-        for i, q in enumerate(senders):
-            lists[q].sort(key=lambda r: (((chips.index(chip_of[r]) - s) * (1 if p % 2 == 0 else -1) + i) % nch, r))
-            for k, r in enumerate(lists[q]):
-                key[r][e] = start[q] + step[q] * (k + 1)
-        helpers = [h for h in senders[1:] if lists[h]]
-        for r in sib[e]:
-            key[r][e] = 2 * T_PLANE + (len(helpers) + 1) * T_CODES
-        mine = [cores[r] for r in lists[c]]
-        near = [cores[r] for r in sib[e]]
-        P = [("hi", helpers, "hp"), ("lo", mine + near, name)]
-        C = [("hi", helpers + near, name), ("lo", mine, name)]
-        prog[c] = [("send", "planes", e, [t for t in P if t[1]]), ("send", "codes", e, [t for t in C if t[1]])]
-        for h in helpers:
-            d = [cores[r] for r in lists[h]]
-            prog[h] = [("wait", "hp"), ("send", "planes", e, [("lo", d, name)]),
-                       ("wait", name), ("send", "codes", e, [("lo", d, name)])]
+        nn = (name, name)
+        A = ("lo", slot[e][e], 1, [(cores[recv[(e, k)][0]], slot[recv[(e, k)][0]][e]) for k in range(len(both[e]))], nn)
+        B = ("lo", slot[e][e], 1, [(cores[r], slot[r][e]) for r in single[e]], nn)
+        L = [(cores[r], slot[r][e]) for r in local[e]]
+        if e in helper:
+            L = [(helper[e], 0)] + L
+        L = ("hi", slot[e][e], 1, L, ("hp", name))
+        key[e][e] = 0.0
+        for k in range(len(both[e])):
+            key[recv[(e, k)][0]][e] = k + 1.0
+        for i, r in enumerate(single[e]):
+            key[r][e] = len(both[e]) + i + 1.0
+        for r in local[e]:
+            key[r][e] = 1.5
+            sem[r][e] = ["hp", name]
+        if e in helper:
+            for i, r in enumerate(hlist[e]):
+                key[r][e] = 3.0 + i
+        first = [t for t in [A] if t[3]]
+        second = [t for t in [B, L] if t[3]]
+        if first:
+            prog[c].append(("send", first, BOTH))
+        if second:
+            prog[c].append(("send", second, BOTH))
+        if e in helper:
+            t = [("lo", 0, 1, [(cores[r], slot[r][e]) for r in hlist[e]], nn)]
+            prog[helper[e]] = [("wait", "hp"), ("send", t, BOTH[:1]), ("wait", name), ("send", t, BOTH[1:])]
+    for r in range(N):
+        if FWD == "each":
+            parts = [(give[r][i:i + 1], None) for i in range(len(give[r]))]
+        elif FWD == "two" and len(give[r]) > 1:
+            parts = [(give[r][:-1], "fw0"), (give[r][-1:], "fw1")]
+        else:
+            parts = [(give[r], "fw0")]
+        for part, name in parts:
+            if not part:
+                continue
+            for (k, e) in part:
+                prog[cores[r]].append(("wait", "a%d" % e))
+            (k0, e0) = part[0]
+            nm = name if name else "a%d" % e0
+            prog[cores[r]].append(("send", [("hi", slot[r][e0], len(part), [(cores[q], slot[q][e0]) for q in recv[(e0, k0)][1]], (nm, nm))], BOTH))
+            for (k, e) in part:
+                for q in recv[(e, k)][1]:
+                    key[q][e] = part[-1][0] + 2.5
+                    sem[q][e] = [nm]
     order = {r: sorted([e for e in range(N) if CNT[r][e] > 0], key=lambda e: (key[r][e], e)) for r in range(N)}
-    return prog, order
+    return prog, slot, sem, order
 
 
 def _bits(m):
@@ -94,8 +156,8 @@ def _bits(m):
 def _mask(topo, cores, core, eng, dsts):
     lo = topo.mask(core, [c for c in cores if topo.chip(c) != topo.chip(core)][0])
     m = lo if eng == "lo" else ~lo
-    for d in dsts:
-        m &= topo.mask(core, d)
+    for (dc, ds) in dsts:
+        m &= topo.mask(core, dc)
     return m
 
 
@@ -104,9 +166,12 @@ def _expect(topo, cores, prog, core):
     for c in prog:
         for st in prog[c]:
             if st[0] == "send":
-                for (eng, dsts, name) in st[3]:
-                    if core in dsts:
-                        tot[name] = tot.get(name, 0) + _bits(_mask(topo, cores, c, eng, dsts))
+                for kind in st[2]:
+                    for (eng, s0, ns, dsts, names) in st[1]:
+                        for (dc, ds) in dsts:
+                            if dc == core:
+                                nm = names[BOTH.index(kind)]
+                                tot[nm] = tot.get(nm, 0) + _bits(_mask(topo, cores, c, eng, dsts))
     return tot
 
 
@@ -118,18 +183,21 @@ def run_steps(g, core, T, topo, prog):
         if st[0] == "wait":
             g.wait_ge(T.sem[st[1]], expect[st[1]])
             continue
-        kind, e = st[1], st[2]
-        if kind == "planes":
-            ap = T.ws[:, e * WCOL:(e + 1) * WCOL]
-        else:
-            ap = T.wq[:, e * WCOL:(e + 1) * WCOL].bitcast(dt.uint8)
-        trs = []
-        for (eng, dsts, name) in st[3]:
-            m = _mask(topo, cores, core, eng, dsts)
-            ids = [DstId(rid=topo.addr(d)[0], pnc=topo.addr(d)[1]) for d in dsts]
-            trs.append(RemoteDMATransfer(dst_ids=ids, dma_engine_mask=m, remote_sem=T.sem[name], srcs=[ap], dsts=[ap for d in dsts]))
-            sent += _bits(m)
-        g.remote_dma_fused(trs, local_sem=T.sem.loc)
+        for kind in st[2]:
+            trs = []
+            for (eng, s0, ns, dsts, names) in st[1]:
+                m = _mask(topo, cores, core, eng, dsts)
+                if kind == "planes":
+                    src = T.ws[:, s0 * WCOL:(s0 + ns) * WCOL]
+                    out = [T.ws[:, ds * WCOL:(ds + ns) * WCOL] for (dc, ds) in dsts]
+                else:
+                    src = T.wq[:, s0 * WCOL:(s0 + ns) * WCOL].bitcast(dt.uint8)
+                    out = [T.wq[:, ds * WCOL:(ds + ns) * WCOL].bitcast(dt.uint8) for (dc, ds) in dsts]
+                ids = [DstId(rid=topo.addr(dc)[0], pnc=topo.addr(dc)[1]) for (dc, ds) in dsts]
+                trs.append(RemoteDMATransfer(dst_ids=ids, dma_engine_mask=m, remote_sem=T.sem[names[BOTH.index(kind)]],
+                                             srcs=[src], dsts=out))
+                sent += _bits(m)
+            g.remote_dma_fused(trs, local_sem=T.sem.loc)
     if sent:
         g.wait_ge(T.sem.loc, sent)
 
@@ -137,7 +205,7 @@ def run_steps(g, core, T, topo, prog):
 def rank_program(g, core, T, topo):
     CNT = T.tables["CNT"]
     cores = list(T.cores)
-    prog, order = make_plan(cores, CNT, topo)
+    prog, slot, sem, order = make_plan(cores, CNT, topo)
     rank = T.rank_of(core)
     if rank is None:
         if core in prog:
@@ -145,12 +213,13 @@ def rank_program(g, core, T, topo):
         return
     expect = _expect(topo, cores, prog, core)
     off = [sum(CNT[rank][:e]) for e in range(len(cores) + 1)]
+    mine = slot[rank][rank]
 
     g.sync.dma_start(T.wb[:], T.w[:]).then_inc(T.sem.lw, 16)
     g.sync.dma_start(T.xb[:], T.x[:]).then_inc(T.sem.lx, 16)
 
     g.vector.wait_ge(T.sem.lw, 16)
-    g.vector.quantize_mx(T.wq[:, rank * WCOL:(rank + 1) * WCOL], T.ws[:, rank * WCOL:(rank + 1) * WCOL], T.wb[:]).then_inc(T.sem.qw, 1)
+    g.vector.quantize_mx(T.wq[:, mine * WCOL:(mine + 1) * WCOL], T.ws[:, mine * WCOL:(mine + 1) * WCOL], T.wb[:]).then_inc(T.sem.qw, 1)
     g.vector.wait_ge(T.sem.lx, 16)
     g.vector.quantize_mx(T.xq[:], T.xs[:], T.xb[:]).then_inc(T.sem.qx, 1)
 
@@ -163,14 +232,16 @@ def rank_program(g, core, T, topo):
         a, n = off[e], CNT[rank][e]
         w0 = a if n >= MINWIN else min(a, NTOK - MINWIN)
         wn = max(n, MINWIN)
+        s = slot[rank][e]
         b = (k % NBANK) * 512
         if e == rank:
             g.tensor.wait_ge(T.sem.qw, 1)
         else:
-            g.tensor.wait_ge(T.sem["a%d" % e], expect["a%d" % e])
+            for nm in sem[rank][e]:
+                g.tensor.wait_ge(T.sem[nm], expect[nm])
         if k >= NBANK:
             g.tensor.wait_ge(T.sem.cp, k - NBANK + 1)
-        g.tensor.matmul_mx(T.ps[:, b:b + wn], T.wq[:, e * WCOL:(e + 1) * WCOL], T.ws[:, e * WCOL:(e + 1) * WCOL],
+        g.tensor.matmul_mx(T.ps[:, b:b + wn], T.wq[:, s * WCOL:(s + 1) * WCOL], T.ws[:, s * WCOL:(s + 1) * WCOL],
                            T.xq[:, w0:w0 + wn], T.xs[:, w0:w0 + wn], True, True).then_inc(T.sem.mm, 1)
         g.vector.wait_ge(T.sem.mm, k + 1)
         g.vector.tensor_copy(T.yb[:, a:a + n], T.ps[:, b + a - w0:b + a - w0 + n]).then_inc(T.sem.cp, 1)
@@ -183,9 +254,9 @@ def rank_program(g, core, T, topo):
             runs[-1][1] = off[e + 1]
         else:
             runs.append([off[e], off[e + 1]])
-    g.sync.wait_ge(T.sem.cp, len(early))
+    g.scalar.wait_ge(T.sem.cp, len(early))
     for (a, b) in runs:
-        g.sync.dma_start(T.y[:, a:b], T.yb[:, a:b]).then_inc(T.sem.st, 16)
+        g.scalar.dma_start(T.y[:, a:b], T.yb[:, a:b]).then_inc(T.sem.st, 16)
     for i in range(nlate):
         e = todo[len(early) + i]
         g.sync.wait_ge(T.sem.cp, len(early) + i + 1)

from concourse.bass import DstId, RemoteDMATransfer
from concourse.mybir import dt

FWD = "two"
HELP = True
LATE = 4

NSLOT = 12
WCOL = 128
NTOK = 512
MINWIN = 128
NBANK = 8
BOTH = ("planes", "codes")

SCRATCH = {
    "wb": ("sbuf", [128, 4 * WCOL], "bfloat16"),
    "xb": ("sbuf", [128, 4 * NTOK], "bfloat16"),
    "wq": ("sbuf", [128, WCOL * NSLOT], "float8_e4m3fn_x4"),
    "ws": ("sbuf", [128, WCOL * NSLOT], "uint8"),
    "xq": ("sbuf", [128, NTOK], "float8_e4m3fn_x4"),
    "xs": ("sbuf", [128, NTOK], "uint8"),
    "ps": ("psum", [128, 512 * NBANK], "float32"),
    "yb": ("sbuf", [128, NTOK], "float32"),
}
SEMAPHORES = ["a%d" % e for e in range(12)] + ["hp", "fw0", "fw1", "lw", "lx", "qw", "qx", "mm", "cp", "st", "loc"]


def make_plan(cores, CNT, topo):
    N = len(cores)
    chip_of = [topo.chip(c) for c in cores]
    chips = sorted(set(chip_of))
    nch = len(chips)
    members = {C: [r for r in range(N) if chip_of[r] == C] for C in chips}
    allc = [c for c in range(topo.CHIPS * topo.CORES_PER_CHIP)]
    both, single, local = {}, {}, {}
    for e in range(N):
        s = chips.index(chip_of[e])
        p = members[chip_of[e]].index(e)
        walk = [chips[(s + k) % nch] for k in range(1, nch)]
        if p % 2:
            walk.reverse()
        both[e], single[e] = [], []
        for C in walk:
            nd = [r for r in members[C] if CNT[r][e] > 0]
            if len(nd) > 1 and FWD != "none":
                both[e].append(nd)
            else:
                for r in nd:
                    single[e].append(r)
        local[e] = [r for r in members[chip_of[e]] if r != e and CNT[r][e] > 0]
    nfwd = [0] * N
    recv = {}
    maxb = max(len(both[e]) for e in range(N))
    for k in range(maxb):
        for e in range(N):
            if k < len(both[e]):
                nd = both[e][k]
                r = min(nd, key=lambda q: (nfwd[q], (q + e) % 2))
                nfwd[r] += 1
                recv[(e, k)] = (r, [q for q in nd if q != r])
    helper, hlist = {}, {}
    if HELP:
        used = set(cores)
        for e in range(N):
            n = len(both[e]) + len(single[e])
            h = min(2 if n >= 5 else 1, len(single[e]))
            if h == 0:
                continue
            take = single[e][len(single[e]) - h:]
            cand = [c for c in allc if topo.chip(c) == chip_of[e] and c not in used
                    and topo.die(c) != topo.die(cores[e])
                    and all(topo.may_write(c, cores[r]) for r in take)]
            if not cand:
                continue
            helper[e] = cand[0]
            used.add(cand[0])
            hlist[e] = take
            single[e] = single[e][:len(single[e]) - h]
    give = {r: [] for r in range(N)}
    for k in range(maxb):
        for e in range(N):
            if (e, k) in recv:
                give[recv[(e, k)][0]].append((k, e))
    slot = {r: {} for r in range(N)}
    for r in range(N):
        for (k, e) in give[r]:
            slot[r][e] = len(slot[r])
    for r in range(N):
        for (k, e) in give[r]:
            for q in recv[(e, k)][1]:
                slot[q][e] = len(slot[q])
    for r in range(N):
        for e in range(N):
            if (CNT[r][e] > 0 or e == r) and e not in slot[r]:
                slot[r][e] = len(slot[r])
    prog = {c: [] for c in cores}
    key = {r: {} for r in range(N)}
    sem = {r: {e: ["a%d" % e] for e in slot[r]} for r in range(N)}
    for e in range(N):
        c = cores[e]
        name = "a%d" % e
        nn = (name, name)
        A = ("lo", slot[e][e], 1, [(cores[recv[(e, k)][0]], slot[recv[(e, k)][0]][e]) for k in range(len(both[e]))], nn)
        B = ("lo", slot[e][e], 1, [(cores[r], slot[r][e]) for r in single[e]], nn)
        L = [(cores[r], slot[r][e]) for r in local[e]]
        if e in helper:
            L = [(helper[e], 0)] + L
        L = ("hi", slot[e][e], 1, L, ("hp", name))
        key[e][e] = 0.0
        for k in range(len(both[e])):
            key[recv[(e, k)][0]][e] = k + 1.0
        for i, r in enumerate(single[e]):
            key[r][e] = len(both[e]) + i + 1.0
        for r in local[e]:
            key[r][e] = 1.5
            sem[r][e] = ["hp", name]
        if e in helper:
            for i, r in enumerate(hlist[e]):
                key[r][e] = 3.0 + i
        first = [t for t in [A] if t[3]]
        second = [t for t in [B, L] if t[3]]
        if first:
            prog[c].append(("send", first, BOTH))
        if second:
            prog[c].append(("send", second, BOTH))
        if e in helper:
            t = [("lo", 0, 1, [(cores[r], slot[r][e]) for r in hlist[e]], nn)]
            prog[helper[e]] = [("wait", "hp"), ("send", t, BOTH[:1]), ("wait", name), ("send", t, BOTH[1:])]
    for r in range(N):
        if FWD == "each":
            parts = [(give[r][i:i + 1], None) for i in range(len(give[r]))]
        elif FWD == "two" and len(give[r]) > 1:
            parts = [(give[r][:-1], "fw0"), (give[r][-1:], "fw1")]
        else:
            parts = [(give[r], "fw0")]
        for part, name in parts:
            if not part:
                continue
            for (k, e) in part:
                prog[cores[r]].append(("wait", "a%d" % e))
            (k0, e0) = part[0]
            nm = name if name else "a%d" % e0
            prog[cores[r]].append(("send", [("hi", slot[r][e0], len(part), [(cores[q], slot[q][e0]) for q in recv[(e0, k0)][1]], (nm, nm))], BOTH))
            for (k, e) in part:
                for q in recv[(e, k)][1]:
                    key[q][e] = part[-1][0] + 2.5
                    sem[q][e] = [nm]
    order = {r: sorted([e for e in range(N) if CNT[r][e] > 0], key=lambda e: (key[r][e], e)) for r in range(N)}
    return prog, slot, sem, order


def _bits(m):
    return bin(m).count("1")


def _mask(topo, cores, core, eng, dsts):
    lo = topo.mask(core, [c for c in cores if topo.chip(c) != topo.chip(core)][0])
    m = lo if eng == "lo" else ~lo
    for (dc, ds) in dsts:
        m &= topo.mask(core, dc)
    return m


def _expect(topo, cores, prog, core):
    tot = {}
    for c in prog:
        for st in prog[c]:
            if st[0] == "send":
                for kind in st[2]:
                    for (eng, s0, ns, dsts, names) in st[1]:
                        for (dc, ds) in dsts:
                            if dc == core:
                                nm = names[BOTH.index(kind)]
                                tot[nm] = tot.get(nm, 0) + _bits(_mask(topo, cores, c, eng, dsts))
    return tot


def run_steps(g, core, T, topo, prog):
    cores = list(T.cores)
    expect = _expect(topo, cores, prog, core)
    sent = 0
    for st in prog[core]:
        if st[0] == "wait":
            g.wait_ge(T.sem[st[1]], expect[st[1]])
            continue
        for kind in st[2]:
            trs = []
            for (eng, s0, ns, dsts, names) in st[1]:
                m = _mask(topo, cores, core, eng, dsts)
                if kind == "planes":
                    src = T.ws[:, s0 * WCOL:(s0 + ns) * WCOL]
                    out = [T.ws[:, ds * WCOL:(ds + ns) * WCOL] for (dc, ds) in dsts]
                else:
                    src = T.wq[:, s0 * WCOL:(s0 + ns) * WCOL].bitcast(dt.uint8)
                    out = [T.wq[:, ds * WCOL:(ds + ns) * WCOL].bitcast(dt.uint8) for (dc, ds) in dsts]
                ids = [DstId(rid=topo.addr(dc)[0], pnc=topo.addr(dc)[1]) for (dc, ds) in dsts]
                trs.append(RemoteDMATransfer(dst_ids=ids, dma_engine_mask=m, remote_sem=T.sem[names[BOTH.index(kind)]],
                                             srcs=[src], dsts=out))
                sent += _bits(m)
            g.remote_dma_fused(trs, local_sem=T.sem.loc)
    if sent:
        g.wait_ge(T.sem.loc, sent)


def rank_program(g, core, T, topo):
    CNT = T.tables["CNT"]
    cores = list(T.cores)
    prog, slot, sem, order = make_plan(cores, CNT, topo)
    rank = T.rank_of(core)
    if rank is None:
        if core in prog:
            run_steps(g, core, T, topo, prog)
        return
    expect = _expect(topo, cores, prog, core)
    off = [sum(CNT[rank][:e]) for e in range(len(cores) + 1)]
    mine = slot[rank][rank]

    g.sync.dma_start(T.wb[:], T.w[:]).then_inc(T.sem.lw, 16)
    g.sync.dma_start(T.xb[:], T.x[:]).then_inc(T.sem.lx, 16)

    g.vector.wait_ge(T.sem.lw, 16)
    g.vector.quantize_mx(T.wq[:, mine * WCOL:(mine + 1) * WCOL], T.ws[:, mine * WCOL:(mine + 1) * WCOL], T.wb[:]).then_inc(T.sem.qw, 1)
    g.vector.wait_ge(T.sem.lx, 16)
    g.vector.quantize_mx(T.xq[:], T.xs[:], T.xb[:]).then_inc(T.sem.qx, 1)

    g.wait_ge(T.sem.qw, 1)
    run_steps(g, core, T, topo, prog)

    g.tensor.wait_ge(T.sem.qx, 1)
    todo = order[rank]
    for k, e in enumerate(todo):
        a, n = off[e], CNT[rank][e]
        w0 = a if n >= MINWIN else min(a, NTOK - MINWIN)
        wn = max(n, MINWIN)
        s = slot[rank][e]
        b = (k % NBANK) * 512
        if e == rank:
            g.tensor.wait_ge(T.sem.qw, 1)
        else:
            for nm in sem[rank][e]:
                g.tensor.wait_ge(T.sem[nm], expect[nm])
        if k >= NBANK:
            g.tensor.wait_ge(T.sem.cp, k - NBANK + 1)
        g.tensor.matmul_mx(T.ps[:, b:b + wn], T.wq[:, s * WCOL:(s + 1) * WCOL], T.ws[:, s * WCOL:(s + 1) * WCOL],
                           T.xq[:, w0:w0 + wn], T.xs[:, w0:w0 + wn], True, True).then_inc(T.sem.mm, 1)
        g.vector.wait_ge(T.sem.mm, k + 1)
        g.vector.tensor_copy(T.yb[:, a:a + n], T.ps[:, b + a - w0:b + a - w0 + n]).then_inc(T.sem.cp, 1)

    nlate = min(LATE, len(todo) - 1)
    early = sorted(todo[:len(todo) - nlate])
    runs = []
    for e in early:
        if runs and runs[-1][1] == off[e]:
            runs[-1][1] = off[e + 1]
        else:
            runs.append([off[e], off[e + 1]])
    g.scalar.wait_ge(T.sem.cp, len(early))
    for (a, b) in runs:
        g.scalar.dma_start(T.y[:, a:b], T.yb[:, a:b]).then_inc(T.sem.st, 16)
    for i in range(nlate):
        e = todo[len(early) + i]
        g.sync.wait_ge(T.sem.cp, len(early) + i + 1)
        g.sync.dma_start(T.y[:, off[e]:off[e + 1]], T.yb[:, off[e]:off[e + 1]]).then_inc(T.sem.st, 16)
    g.sync.wait_ge(T.sem.st, 16 * (len(runs) + nlate))
